import numpy as np, ml_dtypes
CORES = [66,74,82,90,194,202,210,218]
N = 8
NB, B = 4, 256
def setup_inputs(rng):
    return {"x": rng.standard_normal((N, 128, NB * B), dtype=np.float32).astype(ml_dtypes.bfloat16), "wv": (rng.standard_normal((N, 128, 128), dtype=np.float32) / 16).astype(ml_dtypes.bfloat16), "wh": (rng.standard_normal((N, 128, 128), dtype=np.float32) / 16).astype(ml_dtypes.bfloat16)}
def setup_inputs_big(rng):
    d = setup_inputs(rng)
    for k in ("x",): d[k] = (d[k].astype(np.float32) * 1048576.0).astype(d[k].dtype)
    return d
def setup_inputs_small(rng):
    d = setup_inputs(rng)
    for k in ("x",): d[k] = (d[k].astype(np.float32) * (1 / 1048576.0)).astype(d[k].dtype)
    return d
def setup_inputs_apart(rng):
    d = setup_inputs(rng)
    f = (10.0 ** rng.permutation(np.linspace(-1.5, 1.5, N))).astype(np.float32).reshape(N, 1, 1)
    for k in ("x",): d[k] = (d[k].astype(np.float32) * f).astype(d[k].dtype)
    return d
def reference(x, wv, wh):
    X, WV, WH = x.astype(np.float64), wv.astype(np.float64), wh.astype(np.float64)
    h = np.zeros((N, NB, 128, B))
    for r in range(N):
        for c in range(NB):
            a = X[r][:, B * c:B * c + B].copy()
            if r: a += WV[r].T @ h[r - 1][c]
            if c: a += WH[r].T @ h[r][c - 1]
            h[r][c] = np.maximum(a, 0.0)
    return {"y": np.concatenate([h[:, c] for c in range(NB)], axis=2).astype(ml_dtypes.bfloat16)}

@@ -1,0 +1,194 @@
+from concourse.mybir import AluOpType
+
+NB, B, M = 4, 256, 4
+SL = B // M
+WC = 256
+SLOT = WC + NB * SL
+NBANK = 8
+LA = 4
+
+SCRATCH = {
+    "X": ("sbuf", [128, NB * B], "bfloat16"),
+    "SEND": ("sbuf", [128, (M - 1) * SLOT], "bfloat16"),
+    "LAND": ("sbuf", [128, M * SLOT], "bfloat16"),
+    "H": ("sbuf", [128, M * NB * SL], "bfloat16"),
+    "HIN": ("sbuf", [128, NB * SL], "bfloat16"),
+    "YL": ("sbuf", [128, M * NB * SL], "bfloat16"),
+    "Y": ("sbuf", [128, NB * B], "bfloat16"),
+    "Z": ("sbuf", [128, 129], "bfloat16"),
+    "IDD": ("dram", [129, 128], "bfloat16"),
+    "ID": ("sbuf", [128, 128], "bfloat16"),
+    "ZERO": ("sbuf", [128, SL], "float32"),
+}
+for _b in range(NBANK):
+    SCRATCH["P%d" % _b] = ("psum", [128, 512], "float32")
+
+SEMAPHORES = (["ldx", "ldw", "zs", "id1", "id2", "loc", "ycp", "st"]
+              + ["rl%d" % j for j in range(M - 1)] + ["arr%d" % i for i in range(M)]
+              + ["hin%d" % c for c in range(NB)] + ["yar%d" % s for s in range(M)]
+              + ["mm%d" % b for b in range(M * NB)] + ["hd%d" % b for b in range(M * NB)])
+
+
+def _plan(T, topo):
+    st0, st1 = list(T.cores[0:M]), list(T.cores[M:2 * M])
+    sl = {}
+    for s, a in enumerate(st0):
+        sl[a] = s
+    free = list(st0)
+    feeder = {}
+    for b in st1:
+        pick = [a for a in free if topo.same_plane(a, b)] or free
+        feeder[b] = pick[0]
+        sl[b] = sl[pick[0]]
+        free.remove(pick[0])
+    return [st0, st1], sl, feeder
+
+
+def rank_program(g, core, T, topo):
+    rank = T.rank_of(core)
+    if rank is None:
+        return
+    stages, slice_of, feeder = _plan(T, topo)
+    stage, me = rank // M, rank % M
+    mates_ = stages[stage]
+    sl = slice_of[core]
+    S = T.sem
+    v, te, sy, sc = g.vector, g.tensor, g.sync, g.scalar
+    w0 = 128 if rank == 0 else 0
+    nw = 16 * (1 if rank == 0 else 2)
+    sent = [0]
+
+    def send(dst, out, in_, sem):
+        rid, pid = topo.addr(dst, core)
+        mask = topo.mask(core, dst)
+        g.remote_dma(out, in_, sem, S.loc, pid, rid, mask)
+        sent[0] += bin(mask).count("1")
+
+    def eng(src):
+        return bin(topo.mask(src, core)).count("1")
+
+    def hb(i, c, n=1):
+        return T.H[:, (i * NB + c) * SL:(i * NB + c + n) * SL]
+
+    sy.dma_start(T.X[:], T.x[:]).then_inc(S.ldx, 16)
+    if rank != 0:
+        sc.dma_start(T.SEND[:, 0:128], T.wv[:]).then_inc(S.ldw, 16)
+    sc.dma_start(T.SEND[:, 128:256], T.wh[:]).then_inc(S.ldw, 16)
+    v.memset(T.Z[:], 0.0).then_inc(S.zs, 1)
+    v.memset(T.ZERO[:], 0.0).then_inc(S.zs, 1)
+    v.wait_ge(S.zs, 2)
+    v.memset(T.Z[:, 0:1], 1.0).then_inc(S.zs, 1)
+    sc.wait_ge(S.zs, 3)
+    sc.dma_start(T.IDD[:], T.Z[:]).then_inc(S.id1, 16)
+    sc.wait_ge(S.id1, 16)
+    sc.dma_start(T.ID[:], T.IDD[0:128, :]).then_inc(S.id2, 16)
+
+    peers = [(me + d) % M for d in range(1, M)]
+    v.wait_ge(S.ldx, 16)
+    g.wait_ge(S.ldw, nw)
+    for j, p in enumerate(peers):
+        n = 0
+        for c in range(NB):
+            a = j * SLOT + WC + c * SL
+            b = c * B + slice_of[mates_[p]] * SL
+            v.tensor_copy(T.SEND[:, a:a + SL], T.X[:, b:b + SL]).then_inc(S["rl%d" % j], 1)
+            n += 1
+        if j > 0:
+            if j == 1:
+                v.wait_ge(S.ldw, nw)
+            v.tensor_copy(T.SEND[:, j * SLOT + w0:j * SLOT + WC], T.SEND[:, w0:WC]).then_inc(S["rl%d" % j], 1)
+            n += 1
+        g.wait_ge(S["rl%d" % j], n)
+        send(mates_[p], T.LAND[:, me * SLOT + w0:(me + 1) * SLOT], T.SEND[:, j * SLOT + w0:(j + 1) * SLOT], S["arr%d" % me])
+
+    skew = 1 if stage == 0 else 2
+    order = sorted([(i, c) for i in range(M) for c in range(NB)], key=lambda t: (t[0] + skew * t[1], -t[0]))
+    pos = {}
+    for q, t in enumerate(order):
+        pos[t] = q
+    seen = set()
+
+    def tw(name, val):
+        if (name, val) not in seen:
+            seen.add((name, val))
+            te.wait_ge(S[name], val)
+
+    def row_ready(i):
+        if i == me:
+            tw("ldx", 16)
+            tw("ldw", nw)
+        else:
+            tw("arr%d" % i, eng(mates_[i]))
+
+    def wmat(i, which):
+        if i == me:
+            return T.SEND[:, which * 128:which * 128 + 128]
+        return T.LAND[:, i * SLOT + which * 128:i * SLOT + which * 128 + 128]
+
+    def xs(i, c):
+        if i == me:
+            return T.X[:, c * B + sl * SL:c * B + (sl + 1) * SL]
+        return T.LAND[:, i * SLOT + WC + c * SL:i * SLOT + WC + (c + 1) * SL]
+
+    def deps(i, c):
+        d = []
+        if c > 0:
+            d.append((pos[(i, c - 1)], "hd%d" % (i * NB + c - 1), 1, wmat(i, 1), hb(i, c - 1)))
+        if i > 0:
+            d.append((pos[(i - 1, c)], "hd%d" % ((i - 1) * NB + c), 1, wmat(i, 0), hb(i - 1, c)))
+        elif stage == 1:
+            d.append((99, "hin%d" % c, eng(feeder[core]), wmat(i, 0), T.HIN[:, c * SL:(c + 1) * SL]))
+        d.sort(key=lambda t: t[0])
+        return d
+
+    def bank(q):
+        return T["P%d" % (q % NBANK)][:, 0:SL]
+
+    def xmm(q):
+        i, c = order[q]
+        if q >= NBANK:
+            o = order[q - NBANK]
+            tw("hd%d" % (o[0] * NB + o[1]), 1)
+        row_ready(i)
+        tw("id2", 16)
+        te.matmul(bank(q), T.ID[:], xs(i, c), start=True, stop=(len(deps(i, c)) == 0)).then_inc(S["mm%d" % (i * NB + c)], 1)
+
+    nx = 0
+    for p, (i, c) in enumerate(order):
+        while nx <= min(p + LA, len(order) - 1):
+            xmm(nx)
+            nx += 1
+        d = deps(i, c)
+        for n, (_, sem, val, lhsT, rhs) in enumerate(d):
+            tw(sem, val)
+            te.matmul(bank(p), lhsT, rhs, start=False, stop=(n == len(d) - 1)).then_inc(S["mm%d" % (i * NB + c)], 1)
+        v.wait_ge(S["mm%d" % (i * NB + c)], 1 + len(d))
+        v.tensor_tensor(hb(i, c), bank(p), T.ZERO[:], op=AluOpType.max).then_inc(S["hd%d" % (i * NB + c)], 1)
+
+    if stage == 0:
+        nxt = [b for b in stages[1] if feeder[b] == core][0]
+        for c in range(NB):
+            g.wait_ge(S["hd%d" % ((M - 1) * NB + c)], 1)
+            send(nxt, T.HIN[:, c * SL:(c + 1) * SL], hb(M - 1, c), S["hin%d" % c])
+
+    for i in range(M):
+        if i == me:
+            continue
+        for c in range(NB):
+            g.wait_ge(S["hd%d" % (i * NB + c)], 1)
+        send(mates_[i], T.YL[:, sl * NB * SL:(sl + 1) * NB * SL], hb(i, 0, NB), S["yar%d" % sl])
+
+    for c in range(NB):
+        v.wait_ge(S["hd%d" % (me * NB + c)], 1)
+    for c in range(NB):
+        v.tensor_copy(T.Y[:, c * B + sl * SL:c * B + (sl + 1) * SL], hb(me, c)).then_inc(S.ycp, 1)
+    for p in peers:
+        s = slice_of[mates_[p]]
+        v.wait_ge(S["yar%d" % s], eng(mates_[p]))
+        for c in range(NB):
+            v.tensor_copy(T.Y[:, c * B + s * SL:c * B + (s + 1) * SL],
+                          T.YL[:, (s * NB + c) * SL:(s * NB + c + 1) * SL]).then_inc(S.ycp, 1)
+    sy.wait_ge(S.ycp, M * NB)
+    sy.dma_start(T.y[:], T.Y[:]).then_inc(S.st, 16)
+    g.wait_ge(S.loc, sent[0])
+    g.wait_ge(S.st, 16)

@@ -23,9 +23,9 @@ SCRATCH = {
 for _b in range(NBANK):
     SCRATCH["P%d" % _b] = ("psum", [128, 512], "float32")
 
-SEMAPHORES = (["ldx", "ldw", "zs", "id1", "id2", "loc", "ycp", "st"]
+SEMAPHORES = (["ldx", "ldw", "zs", "id1", "id2", "loc", "ycp0", "ycp1", "st0", "st1"]
               + ["rl%d" % j for j in range(M - 1)] + ["arr%d" % i for i in range(M)]
-              + ["hin%d" % c for c in range(NB)] + ["yar%d" % s for s in range(M)]
+              + ["hin%d" % c for c in range(NB)] + ["yar%d_%d" % (ph, s) for ph in range(2) for s in range(M)]
               + ["mm%d" % b for b in range(M * NB)] + ["hd%d" % b for b in range(M * NB)])
 
 
@@ -70,10 +70,12 @@ def rank_program(g, core, T, topo):
     def hb(i, c, n=1):
         return T.H[:, (i * NB + c) * SL:(i * NB + c + n) * SL]
 
-    sy.dma_start(T.X[:], T.x[:]).then_inc(S.ldx, 16)
     if rank != 0:
-        sc.dma_start(T.SEND[:, 0:128], T.wv[:]).then_inc(S.ldw, 16)
-    sc.dma_start(T.SEND[:, 128:256], T.wh[:]).then_inc(S.ldw, 16)
+        sy.dma_start(T.SEND[:, 0:128], T.wv[:]).then_inc(S.ldw, 16)
+        sc.dma_start(T.SEND[:, 128:256], T.wh[:]).then_inc(S.ldw, 16)
+    else:
+        sy.dma_start(T.SEND[:, 128:256], T.wh[:]).then_inc(S.ldw, 16)
+    sy.dma_start(T.X[:], T.x[:]).then_inc(S.ldx, 16)
     v.memset(T.Z[:], 0.0).then_inc(S.zs, 1)
     v.memset(T.ZERO[:], 0.0).then_inc(S.zs, 1)
     v.wait_ge(S.zs, 2)
@@ -84,22 +86,20 @@ def rank_program(g, core, T, topo):
     sc.dma_start(T.ID[:], T.IDD[0:128, :]).then_inc(S.id2, 16)
 
     peers = [(me + d) % M for d in range(1, M)]
-    v.wait_ge(S.ldx, 16)
     g.wait_ge(S.ldw, nw)
+    send(mates_[peers[0]], T.LAND[:, me * SLOT + w0:me * SLOT + WC], T.SEND[:, w0:WC], S["arr%d" % me])
+    v.wait_ge(S.ldw, nw)
+    for j in range(1, M - 1):
+        v.tensor_copy(T.SEND[:, j * SLOT + w0:j * SLOT + WC], T.SEND[:, w0:WC]).then_inc(S["rl%d" % j], 1)
+    v.wait_ge(S.ldx, 16)
     for j, p in enumerate(peers):
-        n = 0
         for c in range(NB):
             a = j * SLOT + WC + c * SL
             b = c * B + slice_of[mates_[p]] * SL
             v.tensor_copy(T.SEND[:, a:a + SL], T.X[:, b:b + SL]).then_inc(S["rl%d" % j], 1)
-            n += 1
-        if j > 0:
-            if j == 1:
-                v.wait_ge(S.ldw, nw)
-            v.tensor_copy(T.SEND[:, j * SLOT + w0:j * SLOT + WC], T.SEND[:, w0:WC]).then_inc(S["rl%d" % j], 1)
-            n += 1
-        g.wait_ge(S["rl%d" % j], n)
-        send(mates_[p], T.LAND[:, me * SLOT + w0:(me + 1) * SLOT], T.SEND[:, j * SLOT + w0:(j + 1) * SLOT], S["arr%d" % me])
+        g.wait_ge(S["rl%d" % j], NB + (1 if j > 0 else 0))
+        f0 = WC if j == 0 else w0
+        send(mates_[p], T.LAND[:, me * SLOT + f0:(me + 1) * SLOT], T.SEND[:, j * SLOT + f0:(j + 1) * SLOT], S["arr%d" % me])
 
     skew = 1 if stage == 0 else 2
     order = sorted([(i, c) for i in range(M) for c in range(NB)], key=lambda t: (t[0] + skew * t[1], -t[0]))
@@ -118,7 +118,7 @@ def rank_program(g, core, T, topo):
             tw("ldx", 16)
             tw("ldw", nw)
         else:
-            tw("arr%d" % i, eng(mates_[i]))
+            tw("arr%d" % i, eng(mates_[i]) * (2 if (i + 1) % M == me else 1))
 
     def wmat(i, which):
         if i == me:
@@ -171,24 +171,29 @@ def rank_program(g, core, T, topo):
             g.wait_ge(S["hd%d" % ((M - 1) * NB + c)], 1)
             send(nxt, T.HIN[:, c * SL:(c + 1) * SL], hb(M - 1, c), S["hin%d" % c])
 
-    for i in range(M):
-        if i == me:
-            continue
-        for c in range(NB):
-            g.wait_ge(S["hd%d" % (i * NB + c)], 1)
-        send(mates_[i], T.YL[:, sl * NB * SL:(sl + 1) * NB * SL], hb(i, 0, NB), S["yar%d" % sl])
+    phases = [(0, NB)] if stage == 0 else [(0, NB // 2), (NB // 2, NB)]
+    for ph, (c0, c1) in enumerate(phases):
+        for i in range(M):
+            if i == me:
+                continue
+            for c in range(c0, c1):
+                g.wait_ge(S["hd%d" % (i * NB + c)], 1)
+            send(mates_[i], T.YL[:, (sl * NB + c0) * SL:(sl * NB + c1) * SL], hb(i, c0, c1 - c0), S["yar%d_%d" % (ph, sl)])
 
-    for c in range(NB):
-        v.wait_ge(S["hd%d" % (me * NB + c)], 1)
-    for c in range(NB):
-        v.tensor_copy(T.Y[:, c * B + sl * SL:c * B + (sl + 1) * SL], hb(me, c)).then_inc(S.ycp, 1)
-    for p in peers:
-        s = slice_of[mates_[p]]
-        v.wait_ge(S["yar%d" % s], eng(mates_[p]))
-        for c in range(NB):
-            v.tensor_copy(T.Y[:, c * B + s * SL:c * B + (s + 1) * SL],
-                          T.YL[:, (s * NB + c) * SL:(s * NB + c + 1) * SL]).then_inc(S.ycp, 1)
-    sy.wait_ge(S.ycp, M * NB)
-    sy.dma_start(T.y[:], T.Y[:]).then_inc(S.st, 16)
+    for ph, (c0, c1) in enumerate(phases):
+        for c in range(c0, c1):
+            v.wait_ge(S["hd%d" % (me * NB + c)], 1)
+        for c in range(c0, c1):
+            v.tensor_copy(T.Y[:, c * B + sl * SL:c * B + (sl + 1) * SL], hb(me, c)).then_inc(S["ycp%d" % ph], 1)
+        for p in peers:
+            s = slice_of[mates_[p]]
+            v.wait_ge(S["yar%d_%d" % (ph, s)], eng(mates_[p]))
+            for c in range(c0, c1):
+                v.tensor_copy(T.Y[:, c * B + s * SL:c * B + (s + 1) * SL],
+                              T.YL[:, (s * NB + c) * SL:(s * NB + c + 1) * SL]).then_inc(S["ycp%d" % ph], 1)
+        q = sy if ph == 0 else sc
+        q.wait_ge(S["ycp%d" % ph], M * (c1 - c0))
+        q.dma_start(T.y[:, c0 * B:c1 * B], T.Y[:, c0 * B:c1 * B]).then_inc(S["st%d" % ph], 16)
     g.wait_ge(S.loc, sent[0])
-    g.wait_ge(S.st, 16)
+    for ph in range(len(phases)):
+        g.wait_ge(S["st%d" % ph], 16)

@@ -1,11 +1,11 @@
-from concourse.mybir import AluOpType
+from concourse.mybir import AluOpType, ActivationFunctionType
 
 NB, B, M = 4, 256, 4
 SL = B // M
 WC = 256
 SLOT = WC + NB * SL
 NBANK = 8
-LA = 4
+LA = 5
 
 SCRATCH = {
     "X": ("sbuf", [128, NB * B], "bfloat16"),
@@ -15,17 +15,16 @@ SCRATCH = {
     "HIN": ("sbuf", [128, NB * SL], "bfloat16"),
     "YL": ("sbuf", [128, M * NB * SL], "bfloat16"),
     "Y": ("sbuf", [128, NB * B], "bfloat16"),
-    "Z": ("sbuf", [128, 129], "bfloat16"),
-    "IDD": ("dram", [129, 128], "bfloat16"),
+    "ONES": ("sbuf", [128, 128], "bfloat16"),
     "ID": ("sbuf", [128, 128], "bfloat16"),
     "ZERO": ("sbuf", [128, SL], "float32"),
 }
 for _b in range(NBANK):
     SCRATCH["P%d" % _b] = ("psum", [128, 512], "float32")
 
-SEMAPHORES = (["ldx", "ldw", "zs", "id1", "id2", "loc", "ycp0", "ycp1", "st0", "st1"]
+SEMAPHORES = (["ldx", "ldw", "zs", "on", "id2", "loc", "ycp", "st0", "st1"]
               + ["rl%d" % j for j in range(M - 1)] + ["arr%d" % i for i in range(M)]
-              + ["hin%d" % c for c in range(NB)] + ["yar%d_%d" % (ph, s) for ph in range(2) for s in range(M)]
+              + ["hin%d" % c for c in range(NB)] + ["yar%d_%d" % (ph, s) for ph in range(3) for s in range(M)]
               + ["mm%d" % b for b in range(M * NB)] + ["hd%d" % b for b in range(M * NB)])
 
 
@@ -54,8 +53,10 @@ def rank_program(g, core, T, topo):
     sl = slice_of[core]
     S = T.sem
     v, te, sy, sc = g.vector, g.tensor, g.sync, g.scalar
+    COPY = ActivationFunctionType.Copy
     w0 = 128 if rank == 0 else 0
     nw = 16 * (1 if rank == 0 else 2)
+    direct = stage == 1
     sent = [0]
 
     def send(dst, out, in_, sem):
@@ -67,8 +68,26 @@ def rank_program(g, core, T, topo):
     def eng(src):
         return bin(topo.mask(src, core)).count("1")
 
+    def gorder(row):
+        a = mates_[row]
+
+        def near(p):
+            b = mates_[p]
+            return 2 if topo.mates(a, b) else (1 if topo.same_plane(a, b) else 0)
+        return sorted([p for p in range(M) if p != row], key=lambda p: (near(p), p))
+
+    def yb(s, c):
+        return T.Y[:, c * B + s * SL:c * B + (s + 1) * SL]
+
     def hb(i, c, n=1):
+        if i == me and direct:
+            return yb(sl, c)
         return T.H[:, (i * NB + c) * SL:(i * NB + c + n) * SL]
+
+    def copy(q, out, in_):
+        if q is v:
+            return v.tensor_copy(out, in_)
+        return sc.activation(out, in_, COPY)
 
     if rank != 0:
         sy.dma_start(T.SEND[:, 0:128], T.wv[:]).then_inc(S.ldw, 16)
@@ -76,27 +95,25 @@ def rank_program(g, core, T, topo):
     else:
         sy.dma_start(T.SEND[:, 128:256], T.wh[:]).then_inc(S.ldw, 16)
     sy.dma_start(T.X[:], T.x[:]).then_inc(S.ldx, 16)
-    v.memset(T.Z[:], 0.0).then_inc(S.zs, 1)
+    v.memset(T.ONES[:], 1.0).then_inc(S.on, 1)
     v.memset(T.ZERO[:], 0.0).then_inc(S.zs, 1)
-    v.wait_ge(S.zs, 2)
-    v.memset(T.Z[:, 0:1], 1.0).then_inc(S.zs, 1)
-    sc.wait_ge(S.zs, 3)
-    sc.dma_start(T.IDD[:], T.Z[:]).then_inc(S.id1, 16)
-    sc.wait_ge(S.id1, 16)
-    sc.dma_start(T.ID[:], T.IDD[0:128, :]).then_inc(S.id2, 16)
+    g.wait_ge(S.on, 1)
+    g.affine_select(T.ID[:], T.ONES[:], [[-1, 128]], AluOpType.is_equal, 0.0, 0, 1).then_inc(S.id2, 1)
 
-    peers = [(me + d) % M for d in range(1, M)]
+    peers = gorder(me)
     g.wait_ge(S.ldw, nw)
     send(mates_[peers[0]], T.LAND[:, me * SLOT + w0:me * SLOT + WC], T.SEND[:, w0:WC], S["arr%d" % me])
-    v.wait_ge(S.ldw, nw)
-    for j in range(1, M - 1):
-        v.tensor_copy(T.SEND[:, j * SLOT + w0:j * SLOT + WC], T.SEND[:, w0:WC]).then_inc(S["rl%d" % j], 1)
+    for j, q in ((1, v), (2, sc)):
+        q.wait_ge(S.ldw, nw)
+        copy(q, T.SEND[:, j * SLOT + w0:j * SLOT + WC], T.SEND[:, w0:WC]).then_inc(S["rl%d" % j], 1)
     v.wait_ge(S.ldx, 16)
+    sc.wait_ge(S.ldx, 16)
     for j, p in enumerate(peers):
         for c in range(NB):
             a = j * SLOT + WC + c * SL
             b = c * B + slice_of[mates_[p]] * SL
-            v.tensor_copy(T.SEND[:, a:a + SL], T.X[:, b:b + SL]).then_inc(S["rl%d" % j], 1)
+            copy(v if c < NB // 2 else sc, T.SEND[:, a:a + SL], T.X[:, b:b + SL]).then_inc(S["rl%d" % j], 1)
+    for j, p in enumerate(peers):
         g.wait_ge(S["rl%d" % j], NB + (1 if j > 0 else 0))
         f0 = WC if j == 0 else w0
         send(mates_[p], T.LAND[:, me * SLOT + f0:(me + 1) * SLOT], T.SEND[:, j * SLOT + f0:(j + 1) * SLOT], S["arr%d" % me])
@@ -113,12 +130,15 @@ def rank_program(g, core, T, topo):
             seen.add((name, val))
             te.wait_ge(S[name], val)
 
+    def turn(i):
+        return 0 if i == me else 1 + gorder(i).index(me)
+
     def row_ready(i):
         if i == me:
             tw("ldx", 16)
             tw("ldw", nw)
         else:
-            tw("arr%d" % i, eng(mates_[i]) * (2 if (i + 1) % M == me else 1))
+            tw("arr%d" % i, eng(mates_[i]) * (2 if gorder(i).index(me) == 0 else 1))
 
     def wmat(i, which):
         if i == me:
@@ -150,10 +170,13 @@ def rank_program(g, core, T, topo):
             o = order[q - NBANK]
             tw("hd%d" % (o[0] * NB + o[1]), 1)
         row_ready(i)
-        tw("id2", 16)
+        tw("id2", 1)
         te.matmul(bank(q), T.ID[:], xs(i, c), start=True, stop=(len(deps(i, c)) == 0)).then_inc(S["mm%d" % (i * NB + c)], 1)
 
-    nx = 0
+    for q in sorted(range(LA + 1), key=lambda q: (turn(order[q][0]), q)):
+        xmm(q)
+    nx = LA + 1
+    v.wait_ge(S.zs, 1)
     for p, (i, c) in enumerate(order):
         while nx <= min(p + LA, len(order) - 1):
             xmm(nx)
@@ -171,29 +194,43 @@ def rank_program(g, core, T, topo):
             g.wait_ge(S["hd%d" % ((M - 1) * NB + c)], 1)
             send(nxt, T.HIN[:, c * SL:(c + 1) * SL], hb(M - 1, c), S["hin%d" % c])
 
-    phases = [(0, NB)] if stage == 0 else [(0, NB // 2), (NB // 2, NB)]
-    for ph, (c0, c1) in enumerate(phases):
-        for i in range(M):
-            if i == me:
-                continue
-            for c in range(c0, c1):
-                g.wait_ge(S["hd%d" % (i * NB + c)], 1)
-            send(mates_[i], T.YL[:, (sl * NB + c0) * SL:(sl * NB + c1) * SL], hb(i, c0, c1 - c0), S["yar%d_%d" % (ph, sl)])
+    phases = [(0, NB)] if stage == 0 else [(0, NB // 2)] + [(c, c + 1) for c in range(NB // 2, NB)]
+    others = [i for i in range(M) if i != me]
+    for _, ph, i in sorted((pos[(i, c1 - 1)], ph, i) for ph, (c0, c1) in enumerate(phases) for i in others):
+        c0, c1 = phases[ph]
+        for c in range(c0, c1):
+            g.wait_ge(S["hd%d" % (i * NB + c)], 1)
+        out = yb(sl, c0) if c1 - c0 == 1 else T.YL[:, (sl * NB + c0) * SL:(sl * NB + c1) * SL]
+        send(mates_[i], out, hb(i, c0, c1 - c0), S["yar%d_%d" % (ph, sl)])
 
-    for ph, (c0, c1) in enumerate(phases):
+    c0, c1 = phases[0]
+    mid = (c0 + c1) // 2
+    share = ((sc, c0, c1),) if direct else ((v, c0, mid), (sc, mid, c1))
+    ncp = 0
+    for p in ([] if direct else [me]) + others:
+        s = slice_of[mates_[p]]
+        for q, a, b in share:
+            if p != me:
+                q.wait_ge(S["yar0_%d" % s], eng(mates_[p]))
+            for c in range(a, b):
+                if p == me:
+                    q.wait_ge(S["hd%d" % (me * NB + c)], 1)
+                src = hb(me, c) if p == me else T.YL[:, (s * NB + c) * SL:(s * NB + c + 1) * SL]
+                copy(q, yb(s, c), src).then_inc(S.ycp, 1)
+                ncp += 1
+    q = sc if direct else sy
+    if direct:
         for c in range(c0, c1):
-            v.wait_ge(S["hd%d" % (me * NB + c)], 1)
-        for c in range(c0, c1):
-            v.tensor_copy(T.Y[:, c * B + sl * SL:c * B + (sl + 1) * SL], hb(me, c)).then_inc(S["ycp%d" % ph], 1)
-        for p in peers:
-            s = slice_of[mates_[p]]
-            v.wait_ge(S["yar%d_%d" % (ph, s)], eng(mates_[p]))
-            for c in range(c0, c1):
-                v.tensor_copy(T.Y[:, c * B + s * SL:c * B + (s + 1) * SL],
-                              T.YL[:, (s * NB + c) * SL:(s * NB + c + 1) * SL]).then_inc(S["ycp%d" % ph], 1)
-        q = sy if ph == 0 else sc
-        q.wait_ge(S["ycp%d" % ph], M * (c1 - c0))
-        q.dma_start(T.y[:, c0 * B:c1 * B], T.Y[:, c0 * B:c1 * B]).then_inc(S["st%d" % ph], 16)
+            q.wait_ge(S["hd%d" % (me * NB + c)], 1)
+    q.wait_ge(S.ycp, ncp)
+    q.dma_start(T.y[:, c0 * B:c1 * B], T.Y[:, c0 * B:c1 * B]).then_inc(S.st0, 16)
+    if direct:
+        for ph in range(1, len(phases)):
+            sy.wait_ge(S["hd%d" % (me * NB + phases[ph][0])], 1)
+            for p in others:
+                sy.wait_ge(S["yar%d_%d" % (ph, slice_of[mates_[p]])], eng(mates_[p]))
+        sy.dma_start(T.y[:, c1 * B:NB * B], T.Y[:, c1 * B:NB * B]).then_inc(S.st1, 16)
     g.wait_ge(S.loc, sent[0])
-    for ph in range(len(phases)):
-        g.wait_ge(S["st%d" % ph], 16)
+    g.wait_ge(S.st0, 16)
+    if direct:
+        g.wait_ge(S.st1, 16)

@@ -118,8 +118,7 @@ def rank_program(g, core, T, topo):
         f0 = WC if j == 0 else w0
         send(mates_[p], T.LAND[:, me * SLOT + f0:(me + 1) * SLOT], T.SEND[:, j * SLOT + f0:(j + 1) * SLOT], S["arr%d" % me])
 
-    skew = 1 if stage == 0 else 2
-    order = sorted([(i, c) for i in range(M) for c in range(NB)], key=lambda t: (t[0] + skew * t[1], -t[0]))
+    order = sorted([(i, c) for i in range(M) for c in range(NB)], key=lambda t: (t[0] + t[1], -t[0]))
     pos = {}
     for q, t in enumerate(order):
         pos[t] = q

@@ -1,11 +1,13 @@
 from concourse.mybir import AluOpType, ActivationFunctionType
 
 NB, B, M = 4, 256, 4
+HB = NB // 2
 SL = B // M
 WC = 256
 SLOT = WC + NB * SL
-NBANK = 8
-LA = 5
+R1 = WC + HB * SL
+NBANK = 2 * M
+LA = 1
 
 SCRATCH = {
     "X": ("sbuf", [128, NB * B], "bfloat16"),
@@ -22,8 +24,9 @@ SCRATCH = {
 for _b in range(NBANK):
     SCRATCH["P%d" % _b] = ("psum", [128, 512], "float32")
 
-SEMAPHORES = (["ldx", "ldw", "zs", "on", "id2", "loc", "ycp", "st0", "st1"]
-              + ["rl%d" % j for j in range(M - 1)] + ["arr%d" % i for i in range(M)]
+SEMAPHORES = (["ldx0", "ldx1", "ldw", "zs", "on", "id2", "loc", "ycp", "st0", "st1", "st2"]
+              + ["rl%d_%d" % (r, j) for r in range(2) for j in range(M - 1)]
+              + ["arr%d" % i for i in range(M)] + ["arb%d" % i for i in range(M)]
               + ["hin%d" % c for c in range(NB)] + ["yar%d_%d" % (ph, s) for ph in range(3) for s in range(M)]
               + ["mm%d" % b for b in range(M * NB)] + ["hd%d" % b for b in range(M * NB)])
 
@@ -94,7 +97,8 @@ def rank_program(g, core, T, topo):
         sc.dma_start(T.SEND[:, 128:256], T.wh[:]).then_inc(S.ldw, 16)
     else:
         sy.dma_start(T.SEND[:, 128:256], T.wh[:]).then_inc(S.ldw, 16)
-    sy.dma_start(T.X[:], T.x[:]).then_inc(S.ldx, 16)
+    for r in range(2):
+        sy.dma_start(T.X[:, r * HB * B:(r + 1) * HB * B], T.x[:, r * HB * B:(r + 1) * HB * B]).then_inc(S["ldx%d" % r], 16)
     v.memset(T.ONES[:], 1.0).then_inc(S.on, 1)
     v.memset(T.ZERO[:], 0.0).then_inc(S.zs, 1)
     g.wait_ge(S.on, 1)
@@ -105,18 +109,22 @@ def rank_program(g, core, T, topo):
     send(mates_[peers[0]], T.LAND[:, me * SLOT + w0:me * SLOT + WC], T.SEND[:, w0:WC], S["arr%d" % me])
     for j, q in ((1, v), (2, sc)):
         q.wait_ge(S.ldw, nw)
-        copy(q, T.SEND[:, j * SLOT + w0:j * SLOT + WC], T.SEND[:, w0:WC]).then_inc(S["rl%d" % j], 1)
-    v.wait_ge(S.ldx, 16)
-    sc.wait_ge(S.ldx, 16)
+        copy(q, T.SEND[:, j * SLOT + w0:j * SLOT + WC], T.SEND[:, w0:WC]).then_inc(S["rl0_%d" % j], 1)
+    for r in range(2):
+        v.wait_ge(S["ldx%d" % r], 16)
+        sc.wait_ge(S["ldx%d" % r], 16)
+        for j, p in enumerate(peers):
+            for c in range(r * HB, (r + 1) * HB):
+                a = j * SLOT + WC + c * SL
+                b = c * B + slice_of[mates_[p]] * SL
+                copy(v if c % 2 == 0 else sc, T.SEND[:, a:a + SL], T.X[:, b:b + SL]).then_inc(S["rl%d_%d" % (r, j)], 1)
     for j, p in enumerate(peers):
-        for c in range(NB):
-            a = j * SLOT + WC + c * SL
-            b = c * B + slice_of[mates_[p]] * SL
-            copy(v if c < NB // 2 else sc, T.SEND[:, a:a + SL], T.X[:, b:b + SL]).then_inc(S["rl%d" % j], 1)
-    for j, p in enumerate(peers):
-        g.wait_ge(S["rl%d" % j], NB + (1 if j > 0 else 0))
+        g.wait_ge(S["rl0_%d" % j], HB + (1 if j > 0 else 0))
         f0 = WC if j == 0 else w0
-        send(mates_[p], T.LAND[:, me * SLOT + f0:(me + 1) * SLOT], T.SEND[:, j * SLOT + f0:(j + 1) * SLOT], S["arr%d" % me])
+        send(mates_[p], T.LAND[:, me * SLOT + f0:me * SLOT + R1], T.SEND[:, j * SLOT + f0:j * SLOT + R1], S["arr%d" % me])
+    for j, p in enumerate(peers):
+        g.wait_ge(S["rl1_%d" % j], HB)
+        send(mates_[p], T.LAND[:, me * SLOT + R1:(me + 1) * SLOT], T.SEND[:, j * SLOT + R1:(j + 1) * SLOT], S["arb%d" % me])
 
     order = sorted([(i, c) for i in range(M) for c in range(NB)], key=lambda t: (t[0] + t[1], -t[0]))
     pos = {}
@@ -132,12 +140,14 @@ def rank_program(g, core, T, topo):
     def turn(i):
         return 0 if i == me else 1 + gorder(i).index(me)
 
-    def row_ready(i):
+    def row_ready(i, c):
         if i == me:
-            tw("ldx", 16)
+            tw("ldx%d" % (c // HB), 16)
             tw("ldw", nw)
         else:
             tw("arr%d" % i, eng(mates_[i]) * (2 if gorder(i).index(me) == 0 else 1))
+            if c >= HB:
+                tw("arb%d" % i, eng(mates_[i]))
 
     def wmat(i, which):
         if i == me:
@@ -160,32 +170,29 @@ def rank_program(g, core, T, topo):
         d.sort(key=lambda t: t[0])
         return d
 
-    def bank(q):
-        return T["P%d" % (q % NBANK)][:, 0:SL]
+    def bank(i, c):
+        return T["P%d" % (HB * i + c % HB)][:, 0:SL]
 
-    def xmm(q):
-        i, c = order[q]
-        if q >= NBANK:
-            o = order[q - NBANK]
-            tw("hd%d" % (o[0] * NB + o[1]), 1)
-        row_ready(i)
+    def xmm(i, c):
+        if c >= HB:
+            tw("hd%d" % (i * NB + c - HB), 1)
+        row_ready(i, c)
         tw("id2", 1)
-        te.matmul(bank(q), T.ID[:], xs(i, c), start=True, stop=(len(deps(i, c)) == 0)).then_inc(S["mm%d" % (i * NB + c)], 1)
+        te.matmul(bank(i, c), T.ID[:], xs(i, c), start=True, stop=(len(deps(i, c)) == 0)).then_inc(S["mm%d" % (i * NB + c)], 1)
 
-    for q in sorted(range(LA + 1), key=lambda q: (turn(order[q][0]), q)):
-        xmm(q)
-    nx = LA + 1
+    for i, c in sorted([t for t in order if t[1] < HB], key=lambda t: (turn(t[0]), pos[t])):
+        xmm(i, c)
+    later = [t for t in order if t[1] >= HB]
     v.wait_ge(S.zs, 1)
     for p, (i, c) in enumerate(order):
-        while nx <= min(p + LA, len(order) - 1):
-            xmm(nx)
-            nx += 1
+        while later and pos[later[0]] <= p + LA:
+            xmm(*later.pop(0))
         d = deps(i, c)
         for n, (_, sem, val, lhsT, rhs) in enumerate(d):
             tw(sem, val)
-            te.matmul(bank(p), lhsT, rhs, start=False, stop=(n == len(d) - 1)).then_inc(S["mm%d" % (i * NB + c)], 1)
+            te.matmul(bank(i, c), lhsT, rhs, start=False, stop=(n == len(d) - 1)).then_inc(S["mm%d" % (i * NB + c)], 1)
         v.wait_ge(S["mm%d" % (i * NB + c)], 1 + len(d))
-        v.tensor_tensor(hb(i, c), bank(p), T.ZERO[:], op=AluOpType.max).then_inc(S["hd%d" % (i * NB + c)], 1)
+        v.tensor_tensor(hb(i, c), bank(i, c), T.ZERO[:], op=AluOpType.max).then_inc(S["hd%d" % (i * NB + c)], 1)
 
     if stage == 0:
         nxt = [b for b in stages[1] if feeder[b] == core][0]
@@ -224,12 +231,14 @@ def rank_program(g, core, T, topo):
     q.wait_ge(S.ycp, ncp)
     q.dma_start(T.y[:, c0 * B:c1 * B], T.Y[:, c0 * B:c1 * B]).then_inc(S.st0, 16)
     if direct:
-        for ph in range(1, len(phases)):
-            sy.wait_ge(S["hd%d" % (me * NB + phases[ph][0])], 1)
+        for ph, q, sem in ((1, sc, S.st2), (2, sy, S.st1)):
+            c = phases[ph][0]
+            q.wait_ge(S["hd%d" % (me * NB + c)], 1)
             for p in others:
-                sy.wait_ge(S["yar%d_%d" % (ph, slice_of[mates_[p]])], eng(mates_[p]))
-        sy.dma_start(T.y[:, c1 * B:NB * B], T.Y[:, c1 * B:NB * B]).then_inc(S.st1, 16)
+                q.wait_ge(S["yar%d_%d" % (ph, slice_of[mates_[p]])], eng(mates_[p]))
+            q.dma_start(T.y[:, c * B:(c + 1) * B], T.Y[:, c * B:(c + 1) * B]).then_inc(sem, 16)
     g.wait_ge(S.loc, sent[0])
     g.wait_ge(S.st0, 16)
     if direct:
         g.wait_ge(S.st1, 16)
+        g.wait_ge(S.st2, 16)

from concourse.mybir import AluOpType, ActivationFunctionType

NB, B, M = 4, 256, 4
HB = NB // 2
SL = B // M
WC = 256
SLOT = WC + NB * SL
R1 = WC + HB * SL
NBANK = 2 * M
LA = 1

SCRATCH = {
    "X": ("sbuf", [128, NB * B], "bfloat16"),
    "SEND": ("sbuf", [128, (M - 1) * SLOT], "bfloat16"),
    "LAND": ("sbuf", [128, M * SLOT], "bfloat16"),
    "H": ("sbuf", [128, M * NB * SL], "bfloat16"),
    "HIN": ("sbuf", [128, NB * SL], "bfloat16"),
    "YL": ("sbuf", [128, M * NB * SL], "bfloat16"),
    "Y": ("sbuf", [128, NB * B], "bfloat16"),
    "ONES": ("sbuf", [128, 128], "bfloat16"),
    "ID": ("sbuf", [128, 128], "bfloat16"),
    "ZERO": ("sbuf", [128, SL], "float32"),
}
for _b in range(NBANK):
    SCRATCH["P%d" % _b] = ("psum", [128, 512], "float32")

SEMAPHORES = (["ldx0", "ldx1", "ldw", "zs", "on", "id2", "loc", "ycp", "st0", "st1", "st2"]
              + ["rl%d_%d" % (r, j) for r in range(2) for j in range(M - 1)]
              + ["arr%d" % i for i in range(M)] + ["arb%d" % i for i in range(M)]
              + ["hin%d" % c for c in range(NB)] + ["yar%d_%d" % (ph, s) for ph in range(3) for s in range(M)]
              + ["mm%d" % b for b in range(M * NB)] + ["hd%d" % b for b in range(M * NB)])


def _plan(T, topo):
    st0, st1 = list(T.cores[0:M]), list(T.cores[M:2 * M])
    sl = {}
    for s, a in enumerate(st0):
        sl[a] = s
    free = list(st0)
    feeder = {}
    for b in st1:
        pick = [a for a in free if topo.same_plane(a, b)] or free
        feeder[b] = pick[0]
        sl[b] = sl[pick[0]]
        free.remove(pick[0])
    return [st0, st1], sl, feeder


def rank_program(g, core, T, topo):
    rank = T.rank_of(core)
    if rank is None:
        return
    stages, slice_of, feeder = _plan(T, topo)
    stage, me = rank // M, rank % M
    mates_ = stages[stage]
    sl = slice_of[core]
    S = T.sem
    v, te, sy, sc = g.vector, g.tensor, g.sync, g.scalar
    COPY = ActivationFunctionType.Copy
    w0 = 128 if rank == 0 else 0
    nw = 16 * (1 if rank == 0 else 2)
    direct = stage == 1
    sent = [0]

    def send(dst, out, in_, sem):
        rid, pid = topo.addr(dst, core)
        mask = topo.mask(core, dst)
        g.remote_dma(out, in_, sem, S.loc, pid, rid, mask)
        sent[0] += bin(mask).count("1")

    def eng(src):
        return bin(topo.mask(src, core)).count("1")

    def gorder(row):
        a = mates_[row]

        def near(p):
            b = mates_[p]
            return 2 if topo.mates(a, b) else (1 if topo.same_plane(a, b) else 0)
        return sorted([p for p in range(M) if p != row], key=lambda p: (near(p), p))

    def yb(s, c):
        return T.Y[:, c * B + s * SL:c * B + (s + 1) * SL]

    def hb(i, c, n=1):
        if i == me and direct:
            return yb(sl, c)
        return T.H[:, (i * NB + c) * SL:(i * NB + c + n) * SL]

    def copy(q, out, in_):
        if q is v:
            return v.tensor_copy(out, in_)
        return sc.activation(out, in_, COPY)

    if rank != 0:
        sy.dma_start(T.SEND[:, 0:128], T.wv[:]).then_inc(S.ldw, 16)
        sc.dma_start(T.SEND[:, 128:256], T.wh[:]).then_inc(S.ldw, 16)
    else:
        sy.dma_start(T.SEND[:, 128:256], T.wh[:]).then_inc(S.ldw, 16)
    for r in range(2):
        sy.dma_start(T.X[:, r * HB * B:(r + 1) * HB * B], T.x[:, r * HB * B:(r + 1) * HB * B]).then_inc(S["ldx%d" % r], 16)
    v.memset(T.ONES[:], 1.0).then_inc(S.on, 1)
    v.memset(T.ZERO[:], 0.0).then_inc(S.zs, 1)
    g.wait_ge(S.on, 1)
    g.affine_select(T.ID[:], T.ONES[:], [[-1, 128]], AluOpType.is_equal, 0.0, 0, 1).then_inc(S.id2, 1)

    peers = gorder(me)
    g.wait_ge(S.ldw, nw)
    send(mates_[peers[0]], T.LAND[:, me * SLOT + w0:me * SLOT + WC], T.SEND[:, w0:WC], S["arr%d" % me])
    for j, q in ((1, v), (2, sc)):
        q.wait_ge(S.ldw, nw)
        copy(q, T.SEND[:, j * SLOT + w0:j * SLOT + WC], T.SEND[:, w0:WC]).then_inc(S["rl0_%d" % j], 1)
    for r in range(2):
        v.wait_ge(S["ldx%d" % r], 16)
        sc.wait_ge(S["ldx%d" % r], 16)
        for j, p in enumerate(peers):
            for c in range(r * HB, (r + 1) * HB):
                a = j * SLOT + WC + c * SL
                b = c * B + slice_of[mates_[p]] * SL
                copy(v if c % 2 == 0 else sc, T.SEND[:, a:a + SL], T.X[:, b:b + SL]).then_inc(S["rl%d_%d" % (r, j)], 1)
    for j, p in enumerate(peers):
        g.wait_ge(S["rl0_%d" % j], HB + (1 if j > 0 else 0))
        f0 = WC if j == 0 else w0
        send(mates_[p], T.LAND[:, me * SLOT + f0:me * SLOT + R1], T.SEND[:, j * SLOT + f0:j * SLOT + R1], S["arr%d" % me])
    for j, p in enumerate(peers):
        g.wait_ge(S["rl1_%d" % j], HB)
        send(mates_[p], T.LAND[:, me * SLOT + R1:(me + 1) * SLOT], T.SEND[:, j * SLOT + R1:(j + 1) * SLOT], S["arb%d" % me])

    order = sorted([(i, c) for i in range(M) for c in range(NB)], key=lambda t: (t[0] + t[1], -t[0]))
    pos = {}
    for q, t in enumerate(order):
        pos[t] = q
    seen = set()

    def tw(name, val):
        if (name, val) not in seen:
            seen.add((name, val))
            te.wait_ge(S[name], val)

    def turn(i):
        return 0 if i == me else 1 + gorder(i).index(me)

    def row_ready(i, c):
        if i == me:
            tw("ldx%d" % (c // HB), 16)
            tw("ldw", nw)
        else:
            tw("arr%d" % i, eng(mates_[i]) * (2 if gorder(i).index(me) == 0 else 1))
            if c >= HB:
                tw("arb%d" % i, eng(mates_[i]))

    def wmat(i, which):
        if i == me:
            return T.SEND[:, which * 128:which * 128 + 128]
        return T.LAND[:, i * SLOT + which * 128:i * SLOT + which * 128 + 128]

    def xs(i, c):
        if i == me:
            return T.X[:, c * B + sl * SL:c * B + (sl + 1) * SL]
        return T.LAND[:, i * SLOT + WC + c * SL:i * SLOT + WC + (c + 1) * SL]

    def deps(i, c):
        d = []
        if c > 0:
            d.append((pos[(i, c - 1)], "hd%d" % (i * NB + c - 1), 1, wmat(i, 1), hb(i, c - 1)))
        if i > 0:
            d.append((pos[(i - 1, c)], "hd%d" % ((i - 1) * NB + c), 1, wmat(i, 0), hb(i - 1, c)))
        elif stage == 1:
            d.append((99, "hin%d" % c, eng(feeder[core]), wmat(i, 0), T.HIN[:, c * SL:(c + 1) * SL]))
        d.sort(key=lambda t: t[0])
        return d

    def bank(i, c):
        return T["P%d" % (HB * i + c % HB)][:, 0:SL]

    def xmm(i, c):
        if c >= HB:
            tw("hd%d" % (i * NB + c - HB), 1)
        row_ready(i, c)
        tw("id2", 1)
        te.matmul(bank(i, c), T.ID[:], xs(i, c), start=True, stop=(len(deps(i, c)) == 0)).then_inc(S["mm%d" % (i * NB + c)], 1)

    for i, c in sorted([t for t in order if t[1] < HB], key=lambda t: (turn(t[0]), pos[t])):
        xmm(i, c)
    later = [t for t in order if t[1] >= HB]
    v.wait_ge(S.zs, 1)
    for p, (i, c) in enumerate(order):
        while later and pos[later[0]] <= p + LA:
            xmm(*later.pop(0))
        d = deps(i, c)
        for n, (_, sem, val, lhsT, rhs) in enumerate(d):
            tw(sem, val)
            te.matmul(bank(i, c), lhsT, rhs, start=False, stop=(n == len(d) - 1)).then_inc(S["mm%d" % (i * NB + c)], 1)
        v.wait_ge(S["mm%d" % (i * NB + c)], 1 + len(d))
        v.tensor_tensor(hb(i, c), bank(i, c), T.ZERO[:], op=AluOpType.max).then_inc(S["hd%d" % (i * NB + c)], 1)

    if stage == 0:
        nxt = [b for b in stages[1] if feeder[b] == core][0]
        for c in range(NB):
            g.wait_ge(S["hd%d" % ((M - 1) * NB + c)], 1)
            send(nxt, T.HIN[:, c * SL:(c + 1) * SL], hb(M - 1, c), S["hin%d" % c])

    phases = [(0, NB)] if stage == 0 else [(0, NB // 2)] + [(c, c + 1) for c in range(NB // 2, NB)]
    others = [i for i in range(M) if i != me]
    for _, ph, i in sorted((pos[(i, c1 - 1)], ph, i) for ph, (c0, c1) in enumerate(phases) for i in others):
        c0, c1 = phases[ph]
        for c in range(c0, c1):
            g.wait_ge(S["hd%d" % (i * NB + c)], 1)
        out = yb(sl, c0) if c1 - c0 == 1 else T.YL[:, (sl * NB + c0) * SL:(sl * NB + c1) * SL]
        send(mates_[i], out, hb(i, c0, c1 - c0), S["yar%d_%d" % (ph, sl)])

    c0, c1 = phases[0]
    mid = (c0 + c1) // 2
    share = ((sc, c0, c1),) if direct else ((v, c0, mid), (sc, mid, c1))
    ncp = 0
    for p in ([] if direct else [me]) + others:
        s = slice_of[mates_[p]]
        for q, a, b in share:
            if p != me:
                q.wait_ge(S["yar0_%d" % s], eng(mates_[p]))
            for c in range(a, b):
                if p == me:
                    q.wait_ge(S["hd%d" % (me * NB + c)], 1)
                src = hb(me, c) if p == me else T.YL[:, (s * NB + c) * SL:(s * NB + c + 1) * SL]
                copy(q, yb(s, c), src).then_inc(S.ycp, 1)
                ncp += 1
    q = sc if direct else sy
    if direct:
        for c in range(c0, c1):
            q.wait_ge(S["hd%d" % (me * NB + c)], 1)
    q.wait_ge(S.ycp, ncp)
    q.dma_start(T.y[:, c0 * B:c1 * B], T.Y[:, c0 * B:c1 * B]).then_inc(S.st0, 16)
    if direct:
        for ph, q, sem in ((1, sc, S.st2), (2, sy, S.st1)):
            c = phases[ph][0]
            q.wait_ge(S["hd%d" % (me * NB + c)], 1)
            for p in others:
                q.wait_ge(S["yar%d_%d" % (ph, slice_of[mates_[p]])], eng(mates_[p]))
            q.dma_start(T.y[:, c * B:(c + 1) * B], T.Y[:, c * B:(c + 1) * B]).then_inc(sem, 16)
    g.wait_ge(S.loc, sent[0])
    g.wait_ge(S.st0, 16)
    if direct:
        g.wait_ge(S.st1, 16)
        g.wait_ge(S.st2, 16)
